import numpy as np
import ml_dtypes


def mxq(x, axis, fmt="e4m3"):
    dtype, down = {"e4m3": (ml_dtypes.float8_e4m3fn, 7), "e5m2": (ml_dtypes.float8_e5m2, 14)}[fmt]
    v = np.moveaxis(np.asarray(x, np.float32).astype(ml_dtypes.bfloat16).astype(np.float64), axis, -1)
    blocks = v.reshape(v.shape[:-1] + (-1, 32))
    amax = np.abs(blocks).max(-1, keepdims=True)
    byte = np.maximum(np.where(amax > 0, np.frexp(amax)[1] - 1 + 127, 0) - down, 1)
    scale = np.exp2(byte - 127.0)
    codes = (blocks / scale).astype(np.float32).astype(dtype).astype(np.float64)
    return np.moveaxis((codes * scale).reshape(v.shape), -1, axis)


WIDE = False


def mx_kscale(k):
    if not WIDE:
        return np.ones(k)
    levels = np.array([10, -10, 5, -5, 0])
    if k % 512:
        return np.exp2(np.random.permutation(np.resize(levels, k // 32))).repeat(32)
    a = np.empty((k // 512, 16))
    for p in range(k // 512):
        a[p, :8] = np.random.permutation(np.resize(levels, 8))
        for g in range(8):
            far = levels[np.abs(levels - a[p, g]) >= 10]
            a[p, g + 8] = far[np.random.randint(len(far))]
    return np.exp2(a.ravel()).repeat(32)


def f64(x):
    return np.asarray(x).astype(np.float64)


def striped(idx):
    return np.tile(idx.reshape(-1, 16).T, (8, 1)).astype(np.uint16)


def unstriped(offs):
    return offs[:16].T.reshape(-1).astype(np.int64)


def striped8(idx):
    return np.concatenate([x.reshape(-1, 16).T for x in idx]).astype(np.uint16)


def runs(offs, k):
    lists = np.stack([offs[16 * r : 16 * r + 16].T.reshape(-1) for r in range(8)]).astype(np.int64)
    return lists[np.arange(k) % 512 // 64]


def pack_weight(w):
    k, n = w.shape
    w = f64(np.asarray(w, np.float32).astype(ml_dtypes.bfloat16)).reshape(k // 32, 32, n)
    amax = np.abs(w).max(1)
    byte = np.clip(np.where(amax > 0, np.frexp(amax)[1] - 1 + 127 - 7, 1), 1, 254)
    scaled = (w * np.exp2(127.0 - byte)[:, None, :]).reshape(k, n).astype(np.float32)
    words = np.ascontiguousarray(scaled.reshape(k // 512, 128, 4, n).transpose(0, 1, 3, 2)).astype(ml_dtypes.float8_e4m3fn).view(np.uint8)
    return words, np.ascontiguousarray(byte.astype(np.uint8).reshape(k // 512, 16, n))


def unpack_weight(words, scales):
    g, p, n, _ = words.shape
    vals = np.ascontiguousarray(words).view(ml_dtypes.float8_e4m3fn).astype(np.float64) * np.repeat(np.exp2(scales.astype(np.float64) - 127.0), 8, axis=1)[..., None]
    return vals.transpose(0, 1, 3, 2).reshape(g * 512, n)


K, T, S, N, G, H, W, U = 512, 2048, 512, 512, 2048, 512, 256, 1024


def setup_inputs():
    n = np.random.standard_normal
    s = mx_kscale(K)[:, None]
    u = mx_kscale(S)
    packed_xT = pack_weight(n((K, T)) * s)
    packed_dT = pack_weight(n((K, G)) / s)
    perm = np.random.permutation(S)
    perm2 = np.stack([np.random.permutation(U) for _ in range(8)])
    return {
        "x_words": packed_xT[0],
        "x_scales": packed_xT[1],
        "d_words": packed_dT[0],
        "d_scales": packed_dT[1],
        "gn": (np.random.uniform(0.5, 1.5, (H, 1)) * u[:, None]).astype(np.float32),
        "w1": (n((H, N)) / np.sqrt(H) / u[:, None]).astype(np.float32),
        "offs": striped8(np.random.randint(0, T, (8, S))),
        "k1": striped8(np.random.randint(0, G, (8, H))),
        "n1": striped(perm[:W]),
        "n2": striped(perm[W:]),
        "n3": striped8(perm2[:, :S]),
        "n4": striped8(perm2[:, S:]),
        "n5": striped8(np.stack([np.random.permutation(S) for _ in range(8)])),
    }


def reference(x_words, x_scales, d_words, d_scales, gn, w1, offs, k1, n1, n2, n3, n4, n5):
    d_k1 = unpack_weight(d_words, d_scales)[np.arange(K)[:, None], runs(k1, K)]
    xq = unpack_weight(x_words, x_scales)[np.arange(K)[:, None], runs(offs, K)]
    h = 0.0625 * (d_k1.T @ xq)
    pa = h[:, unstriped(n1)]
    pb = h[:, unstriped(n2)]
    rb = pa - pb
    ra = 0.75 * (pa + pb)
    ds = np.zeros((H, S))
    ds[:, unstriped(n1)] = ra
    dt = ds.copy()
    dt[:, unstriped(n2)] = rb
    z = f64(gn) * dt
    h2 = mxq(f64(w1), 0, "e4m3").T @ mxq(z, 0, "e4m3")
    dn = np.minimum(h2, h2[np.arange(N)[:, None], runs(n5, N)])
    up = np.maximum(h2, h2[np.arange(N)[:, None], runs(n5, N)])
    ph = np.zeros((N, U))
    ph[np.arange(N)[:, None], runs(n3, N)] = up
    out = ph.copy()
    out[np.arange(N)[:, None], runs(n4, N)] = dn
    return out

@@ -1,0 +1,236 @@
+from contextlib import ExitStack
+
+import concourse.mybir as mybir
+
+F32 = mybir.dt.float32
+BF16 = mybir.dt.bfloat16
+I32 = mybir.dt.int32
+U32 = mybir.dt.uint32
+U16 = mybir.dt.uint16
+U8 = mybir.dt.uint8
+FP8X4 = mybir.dt.float8_e4m3fn_x4
+ALU = mybir.AluOpType
+COPY = mybir.ActivationFunctionType.Copy
+
+P = 128
+T = 2048
+S = 512
+W = 256
+U = 1024
+FLOPS = 2 * 2 * 512 * 512 * 512
+
+H_SCALE = 0.0625 * 0.75
+UNDO = 1.0 / 0.75
+SCALAR_END = 448
+
+
+def tile_picked_hpqhaarpagmx_none_p_kernel(
+    tc, x_words, x_scales, d_words, d_scales, gn, w1, offs, k1, n1, n2, n3, n4, n5, out
+):
+    nc = tc.nc
+    with ExitStack() as ctx:
+        keep = ctx.enter_context(tc.tile_pool(name="keep", bufs=1))
+        psum = ctx.enter_context(tc.psum_pool(name="psum", bufs=1))
+
+        def load_list(src, name):
+            tile = keep.tile(list(src.shape), U16, name=name)
+            nc.sync.dma_start(tile[:], src)
+            return tile
+
+        def load_words(src, name):
+            tile = keep.tile([P, T], U32, name=name)
+            nc.sync.dma_start(tile[:].bitcast(I32), src[0].rearrange("p n r -> p (n r)").bitcast(I32))
+            return tile
+
+        def load_scales(src, name):
+            tile = keep.tile([P, T], U8, name=name)
+            rows = src[0].bitcast(I32)
+            nc.sync.dma_start(tile[:].bitcast(I32), rows.unsqueeze(1).broadcast_to([16, 8, T // 4]))
+            return tile
+
+        k1_t = load_list(k1, "k1_t")
+        offs_t = load_list(offs, "offs_t")
+        d_stab = load_scales(d_scales, "d_stab")
+        x_stab = load_scales(x_scales, "x_stab")
+        d_wtab = load_words(d_words, "d_wtab")
+        n1_t = load_list(n1, "n1_t")
+        n2_t = load_list(n2, "n2_t")
+        n5_t = load_list(n5, "n5_t")
+        x_wtab = load_words(x_words, "x_wtab")
+        n3_t = load_list(n3, "n3_t")
+        n4_t = load_list(n4, "n4_t")
+        gain = keep.tile([P, 4], F32)
+        nc.scalar.dma_start(gain[:], gn.rearrange("(p t) o -> p (t o)", t=4))
+
+        planes = keep.tile([P, 2 * S], U8, align_bytes=64)
+        nc.gpsimd.memset(planes[:].bitcast(I32), 0)
+        ones = keep.tile([P, W], F32)
+        nc.gpsimd.memset(ones[:], 1.0)
+        undo = keep.tile([P, W], F32)
+        nc.scalar.activation(undo[:], ones[:], COPY, scale=UNDO)
+
+        d_sg = keep.tile([P, S], U8)
+        x_sg = keep.tile([P, S], U8)
+        nc.vector.tensor_copy(d_sg[:], d_stab[:].indirect(k1_t[:]))
+        nc.vector.tensor_copy(x_sg[:], x_stab[:].indirect(offs_t[:]))
+        staged = keep.tile([P, 2 * S], U8, tag="staged_then_w1")
+        nc.vector.tensor_copy(
+            staged[:, 0:S].rearrange("p (t m) -> p m t", t=4), d_sg[:].rearrange("p (m t) -> p m t", t=4)
+        )
+        nc.vector.tensor_copy(staged[:, S : 2 * S].bitcast(I32), x_sg[:].bitcast(I32))
+        for a in range(4):
+            nc.scalar.dma_start(planes[a:P:32, :].bitcast(I32), staged[8 * a : P : 32, :].bitcast(I32))
+
+        w_raw = keep.tile([P, 4, S], F32, tag="staged_then_w1")
+        nc.sync.dma_start(w_raw[:], w1.rearrange("(p j) m -> p j m", j=4))
+
+        d_wg = keep.tile([P, S], U32)
+        x_wg = keep.tile([P, S], U32, align_bytes=64)
+        d_codes = keep.tile([P, S], U32, align_bytes=64)
+        nc.vector.tensor_copy(d_wg[:], d_wtab[:].indirect(k1_t[:]))
+        nc.vector.tensor_copy(
+            d_codes[:].rearrange("p (t m) -> p m t", t=4), d_wg[:].rearrange("p (m t) -> p m t", t=4)
+        )
+        nc.vector.tensor_copy(x_wg[:], x_wtab[:].indirect(offs_t[:]))
+
+        h_ps = [psum.tile([P, S], F32, name=f"bank{t}") for t in range(4)]
+        for t in range(4):
+            cols = slice(t * P, (t + 1) * P)
+            nc.tensor.matmul_mx(
+                h_ps[t][:],
+                lhsT=d_codes[:, cols].bitcast(FP8X4),
+                lhsT_scale=planes[:, cols],
+                rhs=x_wg[:].bitcast(FP8X4),
+                rhs_scale=planes[:, S : 2 * S],
+                start=True,
+                stop=True,
+            )
+
+        h = [keep.tile([P, S], F32, name=f"h{t}") for t in range(4)]
+        dt = [keep.tile([P, S], F32, name=f"dt{t}") for t in range(4)]
+        pa = [keep.tile([P, 2, W], F32, name=f"pa{q}") for q in range(2)]
+        pb = [keep.tile([P, 2, W], F32, name=f"pb{q}") for q in range(2)]
+        diff = [keep.tile([P, 2, W], F32, name=f"diff{q}") for q in range(2)]
+        total = [keep.tile([P, W], F32, name=f"total{q}") for q in range(2)]
+        z_rows = keep.tile([P, 4, S], BF16)
+
+        def gather_v(q):
+            nc.vector.tensor_copy(pa[q][:, 0, :], h[2 * q][:].indirect(n1_t[:]))
+            nc.vector.tensor_copy(pb[q][:, 0, :], h[2 * q][:].indirect(n2_t[:]))
+
+        def gather_s(t):
+            nc.scalar.activation(pa[t // 2][:, t % 2, :], h[t][:].indirect(n1_t[:]), COPY)
+            nc.scalar.activation(pb[t // 2][:, t % 2, :], h[t][:].indirect(n2_t[:]), COPY)
+
+        def combine(q):
+            nc.vector.tensor_tensor(diff[q][:], pa[q][:], pb[q][:], ALU.subtract)
+            nc.vector.tensor_tensor(total[q][:], pa[q][:, 1, :], pb[q][:, 1, :], ALU.add)
+
+        def put_sum_v(q):
+            nc.vector.tensor_tensor(dt[2 * q][:].indirect(n1_t[:]), pa[q][:, 0, :], pb[q][:, 0, :], ALU.add)
+
+        def put_diff_v(q):
+            nc.vector.tensor_tensor(dt[2 * q][:].indirect(n2_t[:]), diff[q][:, 0, :], undo[:], ALU.mult)
+
+        def put_s(q):
+            t = 2 * q + 1
+            nc.scalar.activation(dt[t][:].indirect(n2_t[:]), diff[q][:, 1, :], COPY, scale=UNDO)
+            nc.scalar.activation(dt[t][:].indirect(n1_t[:]), total[q][:], COPY)
+            nc.scalar.activation(z_rows[:, t, :], dt[t][:], COPY, scale=gain[:, t : t + 1])
+
+        def round_v(q):
+            t = 2 * q
+            nc.vector.tensor_scalar(z_rows[:, t, :], dt[t][:], gain[:, t : t + 1], None, ALU.mult)
+
+        nc.vector.tensor_scalar(h[0][:], h_ps[0][:], H_SCALE, None, ALU.mult)
+        nc.scalar.activation(h[1][:], h_ps[1][:], COPY, scale=H_SCALE)
+        gather_v(0)
+        gather_s(1)
+        for t in (2, 3):
+            nc.scalar.activation(h[t][:], h_ps[t][:], COPY, scale=H_SCALE)
+            gather_s(t)
+        put_sum_v(0)
+        combine(0)
+        put_diff_v(0)
+        put_s(0)
+        combine(1)
+        round_v(0)
+        put_diff_v(1)
+
+        w_grouped = keep.tile([P, 4 * S], BF16, align_bytes=64)
+        nc.vector.tensor_copy(
+            w_grouped[:].rearrange("p (t m j) -> p m j t", t=4, j=4),
+            w_raw[:].rearrange("p j (m t) -> p m j t", t=4),
+        )
+        w_codes = keep.tile([P, S], U32, align_bytes=64)
+        w_plane = keep.tile([P, S], U8, align_bytes=64)
+        put_sum_v(1)
+        nc.vector.quantize_mx(w_codes[:].bitcast(FP8X4), w_plane[:], w_grouped[:])
+        put_s(1)
+        round_v(1)
+
+        z_grouped = keep.tile([P, S, 4], BF16, align_bytes=64)
+
+        def views(c0, c1):
+            return (
+                z_grouped[:, c0:c1, :].rearrange("p (c i) t -> p c t i", i=4),
+                z_rows[:, :, c0:c1].rearrange("p t (c i) -> p c t i", i=4),
+            )
+
+        z_codes = keep.tile([P, S], U32, align_bytes=64)
+        z_plane = keep.tile([P, S], U8, align_bytes=64)
+
+        def quantise_half(u):
+            cols = slice(u * W, (u + 1) * W)
+            nc.vector.quantize_mx(
+                z_codes[:, cols].bitcast(FP8X4),
+                z_plane[:, cols],
+                z_grouped[:, cols, :].rearrange("p c t -> p (c t)"),
+            )
+
+        nc.vector.tensor_copy(*views(0, W))
+        nc.scalar.copy(*views(W, SCALAR_END))
+        nc.vector.tensor_copy(*views(SCALAR_END, S))
+        quantise_half(0)
+        quantise_half(1)
+
+        def product(acc, t, cols):
+            rows = slice(t * P, (t + 1) * P)
+            nc.tensor.matmul_mx(
+                acc,
+                lhsT=w_codes[:, rows].bitcast(FP8X4),
+                lhsT_scale=w_plane[:, rows],
+                rhs=z_codes[:, cols].bitcast(FP8X4),
+                rhs_scale=z_plane[:, cols],
+                start=True,
+                stop=True,
+            )
+
+        out_rows = out.rearrange("(p t) w -> t p w", t=4)
+        for t in range(4):
+            y = keep.tile([P, S], F32, name=f"y{t}")
+            if t == 0:
+                left = psum.tile([P, W], F32, name="left")
+                right = psum.tile([P, W], F32, name="right")
+                product(left[:], t, slice(0, W))
+                product(right[:], t, slice(W, S))
+                nc.scalar.copy(y[:, 0:W], left[:])
+                nc.vector.tensor_copy(y[:, W:S], right[:])
+            else:
+                acc = psum.tile([P, S], F32, name=f"bank{t}")
+                product(acc[:], t, slice(0, S))
+                nc.scalar.copy(y[:], acc[:])
+            g = keep.tile([P, S], F32, name=f"g{t}")
+            cuts = [0, P, W, S] if t == 0 else [0, W, S]
+            for c0, c1 in zip(cuts, cuts[1:]):
+                nc.scalar.activation(g[:, c0:c1], y[:].indirect(n5_t[:, c0 // 16 : c1 // 16]), COPY)
+            up = keep.tile([P, S], F32, name=f"up{t}")
+            dn = keep.tile([P, S], F32, name=f"dn{t}")
+            page = keep.tile([P, U], F32, name=f"page{t}")
+            pieces = [(0, P), (P, S)] if t == 0 else [(0, S)]
+            for c0, c1 in pieces:
+                nc.vector.tensor_tensor(up[:, c0:c1], y[:, c0:c1], g[:, c0:c1], ALU.max)
+                nc.vector.tensor_tensor(dn[:, c0:c1], y[:, c0:c1], g[:, c0:c1], ALU.min)
+                nc.vector.tensor_copy(page[:].indirect(n3_t[:, c0 // 16 : c1 // 16]), up[:, c0:c1])
+                nc.vector.tensor_copy(page[:].indirect(n4_t[:, c0 // 16 : c1 // 16]), dn[:, c0:c1])
+            nc.sync.dma_start(out_rows[t], page[:])

@@ -1,6 +1,7 @@
 from contextlib import ExitStack
 
 import concourse.mybir as mybir
+from concourse.masks import make_identity
 
 F32 = mybir.dt.float32
 BF16 = mybir.dt.bfloat16
@@ -11,6 +12,7 @@ U8 = mybir.dt.uint8
 FP8X4 = mybir.dt.float8_e4m3fn_x4
 ALU = mybir.AluOpType
 COPY = mybir.ActivationFunctionType.Copy
+RELU = mybir.ActivationFunctionType.Relu
 
 P = 128
 T = 2048
@@ -49,8 +51,8 @@ def tile_picked_hpqhaarpagmx_none_p_kernel(
             return tile
 
         k1_t = load_list(k1, "k1_t")
-        offs_t = load_list(offs, "offs_t")
         d_stab = load_scales(d_scales, "d_stab")
+        offs_t = load_list(offs, "offs_t")
         x_stab = load_scales(x_scales, "x_stab")
         d_wtab = load_words(d_words, "d_wtab")
         n1_t = load_list(n1, "n1_t")
@@ -64,10 +66,10 @@ def tile_picked_hpqhaarpagmx_none_p_kernel(
 
         planes = keep.tile([P, 2 * S], U8, align_bytes=64)
         nc.gpsimd.memset(planes[:].bitcast(I32), 0)
-        ones = keep.tile([P, W], F32)
-        nc.gpsimd.memset(ones[:], 1.0)
-        undo = keep.tile([P, W], F32)
-        nc.scalar.activation(undo[:], ones[:], COPY, scale=UNDO)
+        ident = keep.tile([P, P], F32)
+        make_identity(nc, ident[:])
+        row_scale = keep.tile([P, 4], F32)
+        nc.scalar.activation(row_scale[:], gain[:], COPY, scale=H_SCALE)
 
         d_sg = keep.tile([P, S], U8)
         x_sg = keep.tile([P, S], U8)
@@ -93,81 +95,72 @@ def tile_picked_hpqhaarpagmx_none_p_kernel(
         )
         nc.vector.tensor_copy(x_wg[:], x_wtab[:].indirect(offs_t[:]))
 
-        h_ps = [psum.tile([P, S], F32, name=f"bank{t}") for t in range(4)]
-        for t in range(4):
-            cols = slice(t * P, (t + 1) * P)
+        def first_product(acc, t, c0, c1):
+            rows = slice(t * P, (t + 1) * P)
             nc.tensor.matmul_mx(
-                h_ps[t][:],
-                lhsT=d_codes[:, cols].bitcast(FP8X4),
-                lhsT_scale=planes[:, cols],
-                rhs=x_wg[:].bitcast(FP8X4),
-                rhs_scale=planes[:, S : 2 * S],
+                acc,
+                lhsT=d_codes[:, rows].bitcast(FP8X4),
+                lhsT_scale=planes[:, rows],
+                rhs=x_wg[:, c0:c1].bitcast(FP8X4),
+                rhs_scale=planes[:, S + c0 : S + c1],
                 start=True,
                 stop=True,
             )
 
+        h0_left = psum.tile([P, W], F32, name="left")
+        h0_right = psum.tile([P, W], F32, name="right")
+        first_product(h0_left[:], 0, 0, W)
+        first_product(h0_right[:], 0, W, S)
+        h_ps = {t: psum.tile([P, S], F32, name=f"bank{t}") for t in range(1, 4)}
+        for t in range(1, 4):
+            first_product(h_ps[t][:], t, 0, S)
+
         h = [keep.tile([P, S], F32, name=f"h{t}") for t in range(4)]
         dt = [keep.tile([P, S], F32, name=f"dt{t}") for t in range(4)]
-        pa = [keep.tile([P, 2, W], F32, name=f"pa{q}") for q in range(2)]
+        pa = [keep.tile([P, 2, W], F32, name=f"pa{q}", align_bytes=64) for q in range(2)]
         pb = [keep.tile([P, 2, W], F32, name=f"pb{q}") for q in range(2)]
         diff = [keep.tile([P, 2, W], F32, name=f"diff{q}") for q in range(2)]
-        total = [keep.tile([P, W], F32, name=f"total{q}") for q in range(2)]
-        z_rows = keep.tile([P, 4, S], BF16)
+        z_rows = keep.tile([P, 4, S], BF16, name="z_rows", align_bytes=64)
 
-        def gather_v(q):
-            nc.vector.tensor_copy(pa[q][:, 0, :], h[2 * q][:].indirect(n1_t[:]))
-            nc.vector.tensor_copy(pb[q][:, 0, :], h[2 * q][:].indirect(n2_t[:]))
+        nc.scalar.activation(h[0][:, 0:W], h0_left[:], COPY, scale=row_scale[:, 0:1])
+        nc.vector.tensor_scalar(h[0][:, W:S], h0_right[:], row_scale[:, 0:1], None, ALU.mult)
+        nc.vector.tensor_copy(pa[0][:, 0, :], h[0][:].indirect(n1_t[:]))
+        nc.vector.tensor_copy(pb[0][:, 0, :], h[0][:].indirect(n2_t[:]))
 
-        def gather_s(t):
-            nc.scalar.activation(pa[t // 2][:, t % 2, :], h[t][:].indirect(n1_t[:]), COPY)
+        def empty_bank(t):
+            nc.scalar.activation(h[t][:], h_ps[t][:], COPY, scale=row_scale[:, t : t + 1])
+
+        empty_bank(1)
+        for t in range(1, 4):
+            if t < 3:
+                empty_bank(t + 1)
+            if t == 1:
+                nc.vector.tensor_copy(pa[0][:, 1, :], h[1][:].indirect(n1_t[:]))
+            else:
+                nc.scalar.activation(pa[1][:, t % 2, :], h[t][:].indirect(n1_t[:]), COPY)
             nc.scalar.activation(pb[t // 2][:, t % 2, :], h[t][:].indirect(n2_t[:]), COPY)
 
-        def combine(q):
-            nc.vector.tensor_tensor(diff[q][:], pa[q][:], pb[q][:], ALU.subtract)
-            nc.vector.tensor_tensor(total[q][:], pa[q][:, 1, :], pb[q][:, 1, :], ALU.add)
+        def put_sum(t):
+            q, u = divmod(t, 2)
+            nc.vector.tensor_tensor(dt[t][:].indirect(n1_t[:]), pa[q][:, u, :], pb[q][:, u, :], ALU.add)
 
-        def put_sum_v(q):
-            nc.vector.tensor_tensor(dt[2 * q][:].indirect(n1_t[:]), pa[q][:, 0, :], pb[q][:, 0, :], ALU.add)
+        for t in range(4):
+            q, u = divmod(t, 2)
+            nc.vector.tensor_tensor(diff[q][:, u, :], pa[q][:, u, :], pb[q][:, u, :], ALU.subtract)
+            put_sum(t)
+        for t in range(4):
+            nc.scalar.activation(dt[t][:].indirect(n2_t[:]), diff[t // 2][:, t % 2, :], COPY, scale=UNDO)
 
-        def put_diff_v(q):
-            nc.vector.tensor_tensor(dt[2 * q][:].indirect(n2_t[:]), diff[q][:, 0, :], undo[:], ALU.mult)
-
-        def put_s(q):
-            t = 2 * q + 1
-            nc.scalar.activation(dt[t][:].indirect(n2_t[:]), diff[q][:, 1, :], COPY, scale=UNDO)
-            nc.scalar.activation(dt[t][:].indirect(n1_t[:]), total[q][:], COPY)
-            nc.scalar.activation(z_rows[:, t, :], dt[t][:], COPY, scale=gain[:, t : t + 1])
-
-        def round_v(q):
-            t = 2 * q
-            nc.vector.tensor_scalar(z_rows[:, t, :], dt[t][:], gain[:, t : t + 1], None, ALU.mult)
-
-        nc.vector.tensor_scalar(h[0][:], h_ps[0][:], H_SCALE, None, ALU.mult)
-        nc.scalar.activation(h[1][:], h_ps[1][:], COPY, scale=H_SCALE)
-        gather_v(0)
-        gather_s(1)
-        for t in (2, 3):
-            nc.scalar.activation(h[t][:], h_ps[t][:], COPY, scale=H_SCALE)
-            gather_s(t)
-        put_sum_v(0)
-        combine(0)
-        put_diff_v(0)
-        put_s(0)
-        combine(1)
-        round_v(0)
-        put_diff_v(1)
-
-        w_grouped = keep.tile([P, 4 * S], BF16, align_bytes=64)
-        nc.vector.tensor_copy(
-            w_grouped[:].rearrange("p (t m j) -> p m j t", t=4, j=4),
-            w_raw[:].rearrange("p j (m t) -> p m j t", t=4),
-        )
+        w_first = keep.tile([P, S], BF16, name="pa1", align_bytes=64)
+        w_view = w_raw[:].rearrange("p j (m t) -> p m j t", t=4)
         w_codes = keep.tile([P, S], U32, align_bytes=64)
         w_plane = keep.tile([P, S], U8, align_bytes=64)
-        put_sum_v(1)
-        nc.vector.quantize_mx(w_codes[:].bitcast(FP8X4), w_plane[:], w_grouped[:])
-        put_s(1)
-        round_v(1)
+        nc.vector.tensor_copy(z_rows[:, 0, :], dt[0][:])
+        nc.vector.tensor_copy(z_rows[:, 1, :], dt[1][:])
+        nc.vector.tensor_copy(w_first[:].rearrange("p (m j) -> p m j", j=4), w_view[:, :, :, 0])
+        nc.vector.tensor_copy(z_rows[:, 2, :], dt[2][:])
+        nc.vector.quantize_mx(w_codes[:, 0:P].bitcast(FP8X4), w_plane[:, 0:P], w_first[:])
+        nc.vector.tensor_copy(z_rows[:, 3, :], dt[3][:])
 
         z_grouped = keep.tile([P, S, 4], BF16, align_bytes=64)
 
@@ -194,6 +187,10 @@ def tile_picked_hpqhaarpagmx_none_p_kernel(
         quantise_half(0)
         quantise_half(1)
 
+        w_rest = keep.tile([P, 3 * S], BF16, name="z_rows", align_bytes=64)
+        nc.vector.tensor_copy(w_rest[:].rearrange("p (t m j) -> p m j t", t=3, j=4), w_view[:, :, :, 1:4])
+        nc.vector.quantize_mx(w_codes[:, P:S].bitcast(FP8X4), w_plane[:, P:S], w_rest[:])
+
         def product(acc, t, cols):
             rows = slice(t * P, (t + 1) * P)
             nc.tensor.matmul_mx(
@@ -207,30 +204,70 @@ def tile_picked_hpqhaarpagmx_none_p_kernel(
             )
 
         out_rows = out.rearrange("(p t) w -> t p w", t=4)
-        for t in range(4):
-            y = keep.tile([P, S], F32, name=f"y{t}")
-            if t == 0:
-                left = psum.tile([P, W], F32, name="left")
-                right = psum.tile([P, W], F32, name="right")
-                product(left[:], t, slice(0, W))
-                product(right[:], t, slice(W, S))
-                nc.scalar.copy(y[:, 0:W], left[:])
-                nc.vector.tensor_copy(y[:, W:S], right[:])
-            else:
-                acc = psum.tile([P, S], F32, name=f"bank{t}")
-                product(acc[:], t, slice(0, S))
-                nc.scalar.copy(y[:], acc[:])
-            g = keep.tile([P, S], F32, name=f"g{t}")
-            cuts = [0, P, W, S] if t == 0 else [0, W, S]
+
+        def fetch(g, y, cuts):
             for c0, c1 in zip(cuts, cuts[1:]):
                 nc.scalar.activation(g[:, c0:c1], y[:].indirect(n5_t[:, c0 // 16 : c1 // 16]), COPY)
-            up = keep.tile([P, S], F32, name=f"up{t}")
-            dn = keep.tile([P, S], F32, name=f"dn{t}")
+
+        y = keep.tile([P, S], F32, name="y0")
+        left = psum.tile([P, W], F32, name="left")
+        right = psum.tile([P, W], F32, name="right")
+        product(left[:], 0, slice(0, W))
+        product(right[:], 0, slice(W, S))
+        nc.scalar.copy(y[:, 0:W], left[:])
+        nc.scalar.copy(y[:, W:S], right[:])
+        g = keep.tile([P, S], F32, name="g0")
+        fetch(g, y, [0, P, W, S])
+        up = keep.tile([P, S], F32)
+        dn = keep.tile([P, S], F32)
+        page = keep.tile([P, U], F32, name="page0")
+        for c0, c1 in [(0, P), (P, S)]:
+            nc.vector.tensor_tensor(up[:, c0:c1], y[:, c0:c1], g[:, c0:c1], ALU.max)
+            nc.vector.tensor_tensor(dn[:, c0:c1], y[:, c0:c1], g[:, c0:c1], ALU.min)
+            nc.vector.tensor_copy(page[:].indirect(n3_t[:, c0 // 16 : c1 // 16]), up[:, c0:c1])
+            nc.vector.tensor_copy(page[:].indirect(n4_t[:, c0 // 16 : c1 // 16]), dn[:, c0:c1])
+        nc.sync.dma_start(out_rows[0], page[:])
+
+        pages = {}
+        fetched = {}
+        rises = {}
+
+        def put_larger(t):
+            acc = psum.tile([P, S], F32, name=f"bank{t}" if t < 3 else "gap_turned")
+            product(acc[:], t, slice(0, S))
+            y = keep.tile([P, S], F32, name=f"y{t}")
+            minus_y = keep.tile([P, S], F32, name=f"minus_y{t}")
+            g = keep.tile([P, S], F32, name=f"g{t}")
+            nc.scalar.copy(y[:], acc[:])
+            nc.scalar.activation(minus_y[:], acc[:], COPY, scale=-1.0)
+            fetch(g, y, [0, W, S])
+            gap_turned = psum.tile([P, S], F32, name="gap_turned")
+            for c in range(4):
+                cols = slice(c * P, (c + 1) * P)
+                nc.tensor.matmul(gap_turned[:, cols], g[:, cols], ident[:], start=True, stop=False, is_transpose=True)
+                nc.tensor.matmul(
+                    gap_turned[:, cols], minus_y[:, cols], ident[:], start=False, stop=True, is_transpose=True
+                )
+            rise_turned = keep.tile([P, S], F32, name=f"rise_turned{t}")
+            nc.scalar.activation(rise_turned[:], gap_turned[:], RELU)
+            rise_ps = psum.tile([P, S], F32, name="rise_ps")
+            for c in range(4):
+                cols = slice(c * P, (c + 1) * P)
+                nc.tensor.transpose(rise_ps[:, cols], rise_turned[:, cols], ident[:])
+            rise = keep.tile([P, S], F32, name=f"rise{t}")
+            nc.scalar.copy(rise[:], rise_ps[:])
             page = keep.tile([P, U], F32, name=f"page{t}")
-            pieces = [(0, P), (P, S)] if t == 0 else [(0, S)]
-            for c0, c1 in pieces:
-                nc.vector.tensor_tensor(up[:, c0:c1], y[:, c0:c1], g[:, c0:c1], ALU.max)
-                nc.vector.tensor_tensor(dn[:, c0:c1], y[:, c0:c1], g[:, c0:c1], ALU.min)
-                nc.vector.tensor_copy(page[:].indirect(n3_t[:, c0 // 16 : c1 // 16]), up[:, c0:c1])
-                nc.vector.tensor_copy(page[:].indirect(n4_t[:, c0 // 16 : c1 // 16]), dn[:, c0:c1])
-            nc.sync.dma_start(out_rows[t], page[:])
+            nc.vector.tensor_tensor(page[:].indirect(n3_t[:]), y[:], rise[:], ALU.add)
+            pages[t], fetched[t], rises[t] = page, g, rise
+
+        def put_smaller(t):
+            fall = keep.tile([P, S], F32, name=f"rise_turned{t + 1}")
+            nc.scalar.activation(fall[:], rises[t][:], COPY, scale=-1.0)
+            nc.vector.tensor_tensor(pages[t][:].indirect(n4_t[:]), fetched[t][:], fall[:], ALU.add)
+            nc.sync.dma_start(out_rows[t], pages[t][:])
+
+        put_larger(1)
+        for t in range(1, 4):
+            if t < 3:
+                put_larger(t + 1)
+            put_smaller(t)

from contextlib import ExitStack

import concourse.mybir as mybir
from concourse.masks import make_identity

F32 = mybir.dt.float32
BF16 = mybir.dt.bfloat16
I32 = mybir.dt.int32
U32 = mybir.dt.uint32
U16 = mybir.dt.uint16
U8 = mybir.dt.uint8
FP8X4 = mybir.dt.float8_e4m3fn_x4
ALU = mybir.AluOpType
COPY = mybir.ActivationFunctionType.Copy
RELU = mybir.ActivationFunctionType.Relu

P = 128
T = 2048
S = 512
W = 256
U = 1024
FLOPS = 2 * 2 * 512 * 512 * 512

H_SCALE = 0.0625 * 0.75
UNDO = 1.0 / 0.75
SCALAR_END = 448


def tile_picked_hpqhaarpagmx_none_p_kernel(
    tc, x_words, x_scales, d_words, d_scales, gn, w1, offs, k1, n1, n2, n3, n4, n5, out
):
    nc = tc.nc
    with ExitStack() as ctx:
        keep = ctx.enter_context(tc.tile_pool(name="keep", bufs=1))
        psum = ctx.enter_context(tc.psum_pool(name="psum", bufs=1))

        def load_list(src, name):
            tile = keep.tile(list(src.shape), U16, name=name)
            nc.sync.dma_start(tile[:], src)
            return tile

        def load_words(src, name):
            tile = keep.tile([P, T], U32, name=name)
            nc.sync.dma_start(tile[:].bitcast(I32), src[0].rearrange("p n r -> p (n r)").bitcast(I32))
            return tile

        def load_scales(src, name):
            tile = keep.tile([P, T], U8, name=name)
            rows = src[0].bitcast(I32)
            nc.sync.dma_start(tile[:].bitcast(I32), rows.unsqueeze(1).broadcast_to([16, 8, T // 4]))
            return tile

        k1_t = load_list(k1, "k1_t")
        d_stab = load_scales(d_scales, "d_stab")
        offs_t = load_list(offs, "offs_t")
        x_stab = load_scales(x_scales, "x_stab")
        d_wtab = load_words(d_words, "d_wtab")
        n1_t = load_list(n1, "n1_t")
        n2_t = load_list(n2, "n2_t")
        n5_t = load_list(n5, "n5_t")
        x_wtab = load_words(x_words, "x_wtab")
        n3_t = load_list(n3, "n3_t")
        n4_t = load_list(n4, "n4_t")
        gain = keep.tile([P, 4], F32)
        nc.scalar.dma_start(gain[:], gn.rearrange("(p t) o -> p (t o)", t=4))

        planes = keep.tile([P, 2 * S], U8, align_bytes=64)
        nc.gpsimd.memset(planes[:].bitcast(I32), 0)
        ident = keep.tile([P, P], F32)
        make_identity(nc, ident[:])
        row_scale = keep.tile([P, 4], F32)
        nc.scalar.activation(row_scale[:], gain[:], COPY, scale=H_SCALE)

        d_sg = keep.tile([P, S], U8)
        x_sg = keep.tile([P, S], U8)
        nc.vector.tensor_copy(d_sg[:], d_stab[:].indirect(k1_t[:]))
        nc.vector.tensor_copy(x_sg[:], x_stab[:].indirect(offs_t[:]))
        staged = keep.tile([P, 2 * S], U8, tag="staged_then_w1")
        nc.vector.tensor_copy(
            staged[:, 0:S].rearrange("p (t m) -> p m t", t=4), d_sg[:].rearrange("p (m t) -> p m t", t=4)
        )
        nc.vector.tensor_copy(staged[:, S : 2 * S].bitcast(I32), x_sg[:].bitcast(I32))
        for a in range(4):
            nc.scalar.dma_start(planes[a:P:32, :].bitcast(I32), staged[8 * a : P : 32, :].bitcast(I32))

        w_raw = keep.tile([P, 4, S], F32, tag="staged_then_w1")
        nc.sync.dma_start(w_raw[:], w1.rearrange("(p j) m -> p j m", j=4))

        d_wg = keep.tile([P, S], U32)
        x_wg = keep.tile([P, S], U32, align_bytes=64)
        d_codes = keep.tile([P, S], U32, align_bytes=64)
        nc.vector.tensor_copy(d_wg[:], d_wtab[:].indirect(k1_t[:]))
        nc.vector.tensor_copy(
            d_codes[:].rearrange("p (t m) -> p m t", t=4), d_wg[:].rearrange("p (m t) -> p m t", t=4)
        )
        nc.vector.tensor_copy(x_wg[:], x_wtab[:].indirect(offs_t[:]))

        def first_product(acc, t, c0, c1):
            rows = slice(t * P, (t + 1) * P)
            nc.tensor.matmul_mx(
                acc,
                lhsT=d_codes[:, rows].bitcast(FP8X4),
                lhsT_scale=planes[:, rows],
                rhs=x_wg[:, c0:c1].bitcast(FP8X4),
                rhs_scale=planes[:, S + c0 : S + c1],
                start=True,
                stop=True,
            )

        h0_left = psum.tile([P, W], F32, name="left")
        h0_right = psum.tile([P, W], F32, name="right")
        first_product(h0_left[:], 0, 0, W)
        first_product(h0_right[:], 0, W, S)
        h_ps = {t: psum.tile([P, S], F32, name=f"bank{t}") for t in range(1, 4)}
        for t in range(1, 4):
            first_product(h_ps[t][:], t, 0, S)

        h = [keep.tile([P, S], F32, name=f"h{t}") for t in range(4)]
        dt = [keep.tile([P, S], F32, name=f"dt{t}") for t in range(4)]
        pa = [keep.tile([P, 2, W], F32, name=f"pa{q}", align_bytes=64) for q in range(2)]
        pb = [keep.tile([P, 2, W], F32, name=f"pb{q}") for q in range(2)]
        diff = [keep.tile([P, 2, W], F32, name=f"diff{q}") for q in range(2)]
        z_rows = keep.tile([P, 4, S], BF16, name="z_rows", align_bytes=64)

        nc.scalar.activation(h[0][:, 0:W], h0_left[:], COPY, scale=row_scale[:, 0:1])
        nc.vector.tensor_scalar(h[0][:, W:S], h0_right[:], row_scale[:, 0:1], None, ALU.mult)
        nc.vector.tensor_copy(pa[0][:, 0, :], h[0][:].indirect(n1_t[:]))
        nc.vector.tensor_copy(pb[0][:, 0, :], h[0][:].indirect(n2_t[:]))

        def empty_bank(t):
            nc.scalar.activation(h[t][:], h_ps[t][:], COPY, scale=row_scale[:, t : t + 1])

        empty_bank(1)
        for t in range(1, 4):
            if t < 3:
                empty_bank(t + 1)
            if t == 1:
                nc.vector.tensor_copy(pa[0][:, 1, :], h[1][:].indirect(n1_t[:]))
            else:
                nc.scalar.activation(pa[1][:, t % 2, :], h[t][:].indirect(n1_t[:]), COPY)
            nc.scalar.activation(pb[t // 2][:, t % 2, :], h[t][:].indirect(n2_t[:]), COPY)

        def put_sum(t):
            q, u = divmod(t, 2)
            nc.vector.tensor_tensor(dt[t][:].indirect(n1_t[:]), pa[q][:, u, :], pb[q][:, u, :], ALU.add)

        for t in range(4):
            q, u = divmod(t, 2)
            nc.vector.tensor_tensor(diff[q][:, u, :], pa[q][:, u, :], pb[q][:, u, :], ALU.subtract)
            put_sum(t)
        for t in range(4):
            nc.scalar.activation(dt[t][:].indirect(n2_t[:]), diff[t // 2][:, t % 2, :], COPY, scale=UNDO)

        w_first = keep.tile([P, S], BF16, name="pa1", align_bytes=64)
        w_view = w_raw[:].rearrange("p j (m t) -> p m j t", t=4)
        w_codes = keep.tile([P, S], U32, align_bytes=64)
        w_plane = keep.tile([P, S], U8, align_bytes=64)
        nc.vector.tensor_copy(z_rows[:, 0, :], dt[0][:])
        nc.vector.tensor_copy(z_rows[:, 1, :], dt[1][:])
        nc.vector.tensor_copy(w_first[:].rearrange("p (m j) -> p m j", j=4), w_view[:, :, :, 0])
        nc.vector.tensor_copy(z_rows[:, 2, :], dt[2][:])
        nc.vector.quantize_mx(w_codes[:, 0:P].bitcast(FP8X4), w_plane[:, 0:P], w_first[:])
        nc.vector.tensor_copy(z_rows[:, 3, :], dt[3][:])

        z_grouped = keep.tile([P, S, 4], BF16, align_bytes=64)

        def views(c0, c1):
            return (
                z_grouped[:, c0:c1, :].rearrange("p (c i) t -> p c t i", i=4),
                z_rows[:, :, c0:c1].rearrange("p t (c i) -> p c t i", i=4),
            )

        z_codes = keep.tile([P, S], U32, align_bytes=64)
        z_plane = keep.tile([P, S], U8, align_bytes=64)

        def quantise_half(u):
            cols = slice(u * W, (u + 1) * W)
            nc.vector.quantize_mx(
                z_codes[:, cols].bitcast(FP8X4),
                z_plane[:, cols],
                z_grouped[:, cols, :].rearrange("p c t -> p (c t)"),
            )

        nc.vector.tensor_copy(*views(0, W))
        nc.scalar.copy(*views(W, SCALAR_END))
        nc.vector.tensor_copy(*views(SCALAR_END, S))
        quantise_half(0)
        quantise_half(1)

        w_rest = keep.tile([P, 3 * S], BF16, name="z_rows", align_bytes=64)
        nc.vector.tensor_copy(w_rest[:].rearrange("p (t m j) -> p m j t", t=3, j=4), w_view[:, :, :, 1:4])
        nc.vector.quantize_mx(w_codes[:, P:S].bitcast(FP8X4), w_plane[:, P:S], w_rest[:])

        def product(acc, t, cols):
            rows = slice(t * P, (t + 1) * P)
            nc.tensor.matmul_mx(
                acc,
                lhsT=w_codes[:, rows].bitcast(FP8X4),
                lhsT_scale=w_plane[:, rows],
                rhs=z_codes[:, cols].bitcast(FP8X4),
                rhs_scale=z_plane[:, cols],
                start=True,
                stop=True,
            )

        out_rows = out.rearrange("(p t) w -> t p w", t=4)

        def fetch(g, y, cuts):
            for c0, c1 in zip(cuts, cuts[1:]):
                nc.scalar.activation(g[:, c0:c1], y[:].indirect(n5_t[:, c0 // 16 : c1 // 16]), COPY)

        y = keep.tile([P, S], F32, name="y0")
        left = psum.tile([P, W], F32, name="left")
        right = psum.tile([P, W], F32, name="right")
        product(left[:], 0, slice(0, W))
        product(right[:], 0, slice(W, S))
        nc.scalar.copy(y[:, 0:W], left[:])
        nc.scalar.copy(y[:, W:S], right[:])
        g = keep.tile([P, S], F32, name="g0")
        fetch(g, y, [0, P, W, S])
        up = keep.tile([P, S], F32)
        dn = keep.tile([P, S], F32)
        page = keep.tile([P, U], F32, name="page0")
        for c0, c1 in [(0, P), (P, S)]:
            nc.vector.tensor_tensor(up[:, c0:c1], y[:, c0:c1], g[:, c0:c1], ALU.max)
            nc.vector.tensor_tensor(dn[:, c0:c1], y[:, c0:c1], g[:, c0:c1], ALU.min)
            nc.vector.tensor_copy(page[:].indirect(n3_t[:, c0 // 16 : c1 // 16]), up[:, c0:c1])
            nc.vector.tensor_copy(page[:].indirect(n4_t[:, c0 // 16 : c1 // 16]), dn[:, c0:c1])
        nc.sync.dma_start(out_rows[0], page[:])

        pages = {}
        fetched = {}
        rises = {}

        def put_larger(t):
            acc = psum.tile([P, S], F32, name=f"bank{t}" if t < 3 else "gap_turned")
            product(acc[:], t, slice(0, S))
            y = keep.tile([P, S], F32, name=f"y{t}")
            minus_y = keep.tile([P, S], F32, name=f"minus_y{t}")
            g = keep.tile([P, S], F32, name=f"g{t}")
            nc.scalar.copy(y[:], acc[:])
            nc.scalar.activation(minus_y[:], acc[:], COPY, scale=-1.0)
            fetch(g, y, [0, W, S])
            gap_turned = psum.tile([P, S], F32, name="gap_turned")
            for c in range(4):
                cols = slice(c * P, (c + 1) * P)
                nc.tensor.matmul(gap_turned[:, cols], g[:, cols], ident[:], start=True, stop=False, is_transpose=True)
                nc.tensor.matmul(
                    gap_turned[:, cols], minus_y[:, cols], ident[:], start=False, stop=True, is_transpose=True
                )
            rise_turned = keep.tile([P, S], F32, name=f"rise_turned{t}")
            nc.scalar.activation(rise_turned[:], gap_turned[:], RELU)
            rise_ps = psum.tile([P, S], F32, name="rise_ps")
            for c in range(4):
                cols = slice(c * P, (c + 1) * P)
                nc.tensor.transpose(rise_ps[:, cols], rise_turned[:, cols], ident[:])
            rise = keep.tile([P, S], F32, name=f"rise{t}")
            nc.scalar.copy(rise[:], rise_ps[:])
            page = keep.tile([P, U], F32, name=f"page{t}")
            nc.vector.tensor_tensor(page[:].indirect(n3_t[:]), y[:], rise[:], ALU.add)
            pages[t], fetched[t], rises[t] = page, g, rise

        def put_smaller(t):
            fall = keep.tile([P, S], F32, name=f"rise_turned{t + 1}")
            nc.scalar.activation(fall[:], rises[t][:], COPY, scale=-1.0)
            nc.vector.tensor_tensor(pages[t][:].indirect(n4_t[:]), fetched[t][:], fall[:], ALU.add)
            nc.sync.dma_start(out_rows[t], pages[t][:])

        put_larger(1)
        for t in range(1, 4):
            if t < 3:
                put_larger(t + 1)
            put_smaller(t)
